import numpy as np
import ml_dtypes


def mxq(x, axis, fmt="e4m3"):
    dtype, down = {"e4m3": (ml_dtypes.float8_e4m3fn, 7), "e5m2": (ml_dtypes.float8_e5m2, 14)}[fmt]
    v = np.moveaxis(np.asarray(x, np.float32).astype(ml_dtypes.bfloat16).astype(np.float64), axis, -1)
    blocks = v.reshape(v.shape[:-1] + (-1, 32))
    amax = np.abs(blocks).max(-1, keepdims=True)
    byte = np.maximum(np.where(amax > 0, np.frexp(amax)[1] - 1 + 127, 0) - down, 1)
    scale = np.exp2(byte - 127.0)
    codes = (blocks / scale).astype(np.float32).astype(dtype).astype(np.float64)
    return np.moveaxis((codes * scale).reshape(v.shape), -1, axis)


WIDE = False


def mx_kscale(k):
    if not WIDE:
        return np.ones(k)
    levels = np.array([10, -10, 5, -5, 0])
    if k % 512:
        return np.exp2(np.random.permutation(np.resize(levels, k // 32))).repeat(32)
    a = np.empty((k // 512, 16))
    for p in range(k // 512):
        a[p, :8] = np.random.permutation(np.resize(levels, 8))
        for g in range(8):
            far = levels[np.abs(levels - a[p, g]) >= 10]
            a[p, g + 8] = far[np.random.randint(len(far))]
    return np.exp2(a.ravel()).repeat(32)


def f64(x):
    return np.asarray(x).astype(np.float64)


def striped(idx):
    return np.tile(idx.reshape(-1, 16).T, (8, 1)).astype(np.uint16)


def unstriped(offs):
    return offs[:16].T.reshape(-1).astype(np.int64)


E2M1 = np.array([0.0, 0.5, 1.0, 1.5, 2.0, 3.0, 4.0, 6.0, -0.0, -0.5, -1.0, -1.5, -2.0, -3.0, -4.0, -6.0])


def pack_weight(w, fmt):
    k, n = w.shape
    w = f64(np.asarray(w, np.float32).astype(ml_dtypes.bfloat16)).reshape(k // 32, 32, n)
    amax = np.abs(w).max(1)
    if fmt == "e4m3":
        byte = np.frexp(amax)[1] - 1 + 127 - 7
    else:
        mant, ex = np.frexp(amax / 6.0)
        byte = np.where(mant > 0.5, ex, ex - 1) + 127
    byte = np.clip(np.where(amax > 0, byte, 1), 1, 254)
    scaled = (w * np.exp2(127.0 - byte)[:, None, :]).reshape(k, n).astype(np.float32)
    by_word = np.ascontiguousarray(scaled.reshape(k // 512, 128, 4, n).transpose(0, 1, 3, 2))
    if fmt == "e4m3":
        words = by_word.astype(ml_dtypes.float8_e4m3fn).view(np.uint8)
    else:
        c = by_word.astype(ml_dtypes.float4_e2m1fn).view(np.uint8) & 0xF
        words = (c[..., 0::2] | (c[..., 1::2] << 4)).reshape(k // 512, 128, 2 * n)
    return np.ascontiguousarray(words), np.ascontiguousarray(byte.astype(np.uint8).reshape(k // 512, 16, n))


def unpack_weight(words, scales, fmt):
    g, _, n = scales.shape
    words = np.ascontiguousarray(words).reshape(g, 128, n, -1)
    if fmt == "e4m3":
        vals = words.view(ml_dtypes.float8_e4m3fn).astype(np.float64)
    else:
        nib = np.empty((g, 128, n, 4), np.uint8)
        nib[..., 0::2] = words & 0xF
        nib[..., 1::2] = words >> 4
        vals = E2M1[nib]
    vals = vals * np.repeat(np.exp2(scales.astype(np.float64) - 127.0), 8, axis=1)[..., None]
    return vals.transpose(0, 1, 3, 2).reshape(g * 512, n)


def gelu(v):
    return 0.5 * v * (1.0 + np.tanh(np.sqrt(2.0 / np.pi) * (v + 0.044715 * v**3)))


K, T, S, H, P, P2, N = 1024, 4096, 1024, 1024, 512, 256, 512

def setup_inputs():
    n = np.random.standard_normal
    s = mx_kscale(K)[:, None]
    u = mx_kscale(H)[:, None]
    d = {}
    d["tab_words"], d["tab_scales"] = pack_weight(n((K, T)) * s, "e4m3")
    d["offs"] = striped(np.random.permutation(T)[:S])
    d["pos1"] = striped(np.random.permutation(S)[:P])
    d["pos2"] = striped(np.random.permutation(P)[:P2])
    d["w1"] = (1.5 * n((K, H)) / K ** 0.5 / s).astype(np.float32)
    d["w2_words"], d["w2_scales"] = pack_weight(0.8 * n((K, H)) / K ** 0.5 / s, "e2m1")
    d["gain"] = (0.8 * np.exp(0.3 * n(H)) * np.sign(n(H)) * u[:, 0]).astype(np.float32)
    d["ws_words"], d["ws_scales"] = pack_weight(n((H, H)) / H ** 0.5 / u * u.T, "e4m3")
    d["ctx"] = (0.9 * n((H, P))).astype(np.float32)
    d["wo"] = (1.2 * n((H, N)) / H ** 0.5 / u).astype(np.float32)
    d["board"] = n((N, P2)).astype(np.float32)
    return d

def reference(tab_words, tab_scales, offs, pos1, pos2, w1, w2_words, w2_scales, gain, ws_words, ws_scales, ctx, wo, board):
    v = unpack_weight(tab_words, tab_scales, "e4m3")[:, unstriped(offs)]
    w2 = unpack_weight(w2_words, w2_scales, "e2m1")
    ws = unpack_weight(ws_words, ws_scales, "e4m3")
    mark = mxq(f64(w1), 0, "e4m3").T @ v
    ground = w2.T @ v
    h = np.square(np.tanh(mark) - ground) * f64(gain)[:, None]
    x1 = h[:, unstriped(pos1)]
    x2 = x1 + f64(ctx) * (ws.T @ mxq(x1, 0, "e4m3"))
    x3 = x2[:, unstriped(pos2)]
    y = mxq(f64(wo), 0, "e4m3").T @ mxq(x3, 0, "e4m3")
    return f64(board) / (1.0 + np.exp(-y))

from contextlib import ExitStack

import concourse.mybir as mybir

K, T, S, H, P1, P2, N = 1024, 4096, 1024, 1024, 512, 256, 512
FLOPS = 2 * (2 * K * H * S + H * H * P1 + H * N * P2)

F32 = mybir.dt.float32
BF16 = mybir.dt.bfloat16
I32 = mybir.dt.int32
U32 = mybir.dt.uint32
U16 = mybir.dt.uint16
U8 = mybir.dt.uint8
FP8X4 = mybir.dt.float8_e4m3fn_x4
FP4X4 = mybir.dt.float4_e2m1fn_x4
ACT = mybir.ActivationFunctionType
ALU = mybir.AluOpType

PART = 128
PACK = 4
KP = PART * PACK
PASSES = 2
BANK = 512
SLOT = 8192
LAG = 2


def tile_list_mark_intent_trunk_kernel(tc, tab_words, tab_scales, offs, pos1, pos2, w1, w2_words, w2_scales,
                                                gain, ws_words, ws_scales, ctx, wo, board, out):
    nc = tc.nc
    with ExitStack() as stack:
        keep = stack.enter_context(tc.tile_pool(name="keep", bufs=1))
        ring = stack.enter_context(tc.tile_pool(name="ring", bufs=2))
        stage = stack.enter_context(tc.tile_pool(name="stage", bufs=1))
        psum = stack.enter_context(tc.psum_pool(name="psum", bufs=4))

        def scalar_copy(out_ap, in_ap):
            nc.scalar.activation(out=out_ap, in_=in_ap, func=ACT.Copy)

        def vector_copy(out_ap, in_ap):
            nc.vector.tensor_copy(out=out_ap, in_=in_ap)

        wsc_raw = keep.tile([PART, PASSES, H], U8, name="wsc_raw", align_bytes=64)
        nc.vector.memset(wsc_raw[:].rearrange("p a c -> p (a c)").bitcast(I32), 0)
        tsc = keep.tile([PART, T], U8, name="tsc", align_bytes=64)
        nc.vector.memset(tsc[32:64, :].bitcast(I32), 0)
        nc.vector.memset(tsc[64:128, :].bitcast(I32), 0)
        v_plane = [keep.tile([PART, S], U8, name=f"v_plane{a}", align_bytes=64) for a in range(PASSES)]
        for a in range(PASSES):
            nc.vector.memset(v_plane[a][:].bitcast(I32), 0)

        offs_t = keep.tile([PART, S // 16], U16, name="offs_t")
        nc.sync.dma_start(offs_t[:], offs)
        nc.sync.dma_start(out=tsc[0:32, :].bitcast(I32), in_=tab_scales.rearrange("a q t -> (a q) t").bitcast(I32))

        def load_rows(w, a, c0, name, slot):
            raw = stage.tile([PART, PACK, KP], F32, name=name, offset=slot * SLOT // 2, align_bytes=64)
            nc.sync.dma_start(out=raw[:], in_=w[a * KP:(a + 1) * KP, c0:c0 + KP].rearrange("(p j) c -> p j c", j=PACK))
            return raw

        def quantize_weight(raw, copy, name):
            grouped = ring.tile([PART, PACK * KP], BF16, name=name + "_bf", tag="wbf", align_bytes=64)
            copy(grouped[:].rearrange("p (t m j) -> p m j t", t=PACK, j=PACK),
                 raw[:].rearrange("p j (m t) -> p m j t", t=PACK))
            codes = keep.tile([PART, KP], U32, name=name + "_codes", tag=name + "_codes", align_bytes=64)
            plane = keep.tile([PART, KP], U8, name=name + "_plane", align_bytes=64)
            nc.vector.quantize_mx(out=codes[:].bitcast(FP8X4), scales=plane[:], in_=grouped[:])
            return codes, plane

        w1_raw = {(a, 0): load_rows(w1, a, 0, f"w1_raw{a}0", 8 + 2 * a) for a in range(PASSES)}

        w2_raw = keep.tile([PART, PASSES, 2 * H], U8, name="w2_raw", align_bytes=64)
        for q in range(4):
            nc.sync.dma_start(out=wsc_raw[32 * q:32 * q + 4, :, :].bitcast(I32),
                              in_=w2_scales[:, 4 * q:4 * q + 4, :].rearrange("a r c -> r a c").bitcast(I32))
        nc.sync.dma_start(out=w2_raw[:].bitcast(I32), in_=w2_words.rearrange("a p c -> p a c").bitcast(I32))

        def load_table(a):
            words = stage.tile([PART, T], U32, name=f"tab{a}", offset=2 * a * SLOT, align_bytes=64)
            nc.sync.dma_start(out=words[:].bitcast(I32), in_=tab_words[a].rearrange("p t i -> p (t i)").bitcast(I32))
            return words

        tab = [load_table(0)]
        for q in range(4):
            nc.sync.dma_start(out=wsc_raw[32 * q + 4:32 * q + 8, :, :].bitcast(I32),
                              in_=ws_scales[:, 4 * q:4 * q + 4, :].rearrange("a r c -> r a c").bitcast(I32))
        tab.append(load_table(1))
        pos1_t = keep.tile([PART, P1 // 16], U16, name="pos1_t")
        nc.sync.dma_start(pos1_t[:], pos1)
        gain_t = keep.tile([PART, PASSES, PACK], F32, name="gain_t")
        nc.sync.dma_start(out=gain_t[:], in_=gain.rearrange("(b p t) -> p b t", b=PASSES, t=PACK))

        gsc = keep.tile([PART, S], U8, name="gsc", align_bytes=64)
        nc.vector.tensor_copy(out=gsc[:], in_=tsc[:].indirect(offs_t[:]))
        for a in range(PASSES):
            for q in range(4):
                row = 16 * a + 4 * q
                nc.gpsimd.dma_start(out=v_plane[a][32 * q:32 * q + 4, :].bitcast(I32), in_=gsc[row:row + 4, :].bitcast(I32))

        w1_q = {(a, 0): quantize_weight(w1_raw[a, 0], scalar_copy, f"w1_{a}0") for a in range(PASSES)}

        w2_p = stage.tile([PART, PASSES * 2 * H], U8, name="w2_p", offset=7 * SLOT - 2048, align_bytes=64)
        nc.vector.tensor_copy(out=w2_p[:].bitcast(U16).rearrange("p (g t m) -> p g m t", t=PACK, m=PART),
                              in_=w2_raw[:].rearrange("p a c -> p (a c)").bitcast(U16).rearrange("p (g m t) -> p g m t", t=PACK, m=PART))
        wsc = keep.tile([PART, PASSES * H], U8, name="wsc", align_bytes=64)
        nc.vector.tensor_copy(out=wsc[:].rearrange("p (g t m) -> p g m t", t=PACK, m=PART),
                              in_=wsc_raw[:].rearrange("p a (b m t) -> p (a b) m t", t=PACK, m=PART))

        v_codes = {}
        for a in range(PASSES):
            for half in range(2):
                codes = keep.tile([PART, BANK], U32, name=f"v_codes{a}{half}", align_bytes=64)
                nc.vector.tensor_copy(out=codes[:], in_=tab[a][:].indirect(offs_t[:, 32 * half:32 * half + 32]))
                v_codes[a, half] = codes

        pos2_t = keep.tile([PART, P2 // 16], U16, name="pos2_t")
        nc.sync.dma_start(pos2_t[:], pos2)
        w1_raw[0, 1] = load_rows(w1, 0, KP, "w1_raw01", 2)
        w1_raw[1, 1] = load_rows(w1, 1, KP, "w1_raw11", 4)
        ws_raw = stage.tile([PART, PASSES, H], U32, name="ws_raw", offset=13 * SLOT // 4, align_bytes=64)
        nc.sync.dma_start(out=ws_raw[:].bitcast(I32), in_=ws_words.rearrange("a p c i -> p a (c i)").bitcast(I32))

        x1 = keep.tile([PART, PASSES * PACK, P1], F32, name="x1")
        x1_codes = [keep.tile([PART, P1], U32, name=f"x1_codes{b}", align_bytes=64) for b in range(PASSES)]
        x1_plane = [keep.tile([PART, P1], U8, name=f"x1_plane{b}", align_bytes=64) for b in range(PASSES)]

        def quantize_columns(x, c0, width, copy, codes, plane, name):
            grouped = ring.tile([PART, PACK * width], BF16, name=name, tag="xbf", align_bytes=64)
            copy(grouped[:].rearrange("p (c i t) -> p c t i", i=4, t=PACK),
                 x[:, :, c0:c0 + width].rearrange("p t (c i) -> p c t i", i=4))
            nc.vector.quantize_mx(out=codes[:, c0:c0 + width].bitcast(FP8X4), scales=plane[:, c0:c0 + width], in_=grouped[:])

        h_tiles = {}

        def pick_inked(i):
            nc.vector.tensor_copy(out=x1[:, i, :], in_=h_tiles[i][:].indirect(pos1_t[:]))

        def first_stage(b, t):
            h = ring.tile([PART, S], F32, name="h", tag="h", bufs=LAG + 2)
            i = b * PACK + t
            h_tiles[i] = h
            for half in range(2):
                cols = slice(half * BANK, (half + 1) * BANK)
                mark = psum.tile([PART, BANK], F32, name="mark", tag="mark")
                ground = psum.tile([PART, BANK], F32, name="ground", tag="ground")
                for a in range(PASSES):
                    codes, plane = w1_q[a, b]
                    nc.tensor.matmul_mx(out=mark[:], lhsT=codes[:, t * PART:(t + 1) * PART].bitcast(FP8X4),
                                        lhsT_scale=plane[:, t * PART:(t + 1) * PART],
                                        rhs=v_codes[a, half][:].bitcast(FP8X4), rhs_scale=v_plane[a][:, cols],
                                        start=(a == 0), stop=(a == PASSES - 1))
                for a in range(PASSES):
                    c0 = a * H + b * KP + t * PART
                    nc.tensor.matmul_mx(out=ground[:], lhsT=w2_p[:, 2 * c0:2 * (c0 + PART)].bitcast(FP4X4),
                                        lhsT_scale=wsc[:, c0:c0 + PART],
                                        rhs=v_codes[a, half][:].bitcast(FP8X4), rhs_scale=v_plane[a][:, cols],
                                        start=(a == 0), stop=(a == PASSES - 1))
                if half == 0 and i >= LAG:
                    bounded = x1[:, i - LAG, :]
                else:
                    spare = ring.tile([PART, BANK], F32, name="spare", tag="spare", bufs=3)
                    bounded = spare[:]
                nc.scalar.activation(out=bounded, in_=mark[:], func=ACT.Tanh)
                nc.vector.tensor_tensor(out=h[:, cols], in0=bounded, in1=ground[:], op=ALU.subtract)
            nc.scalar.activation(out=h[:], in_=h[:], func=ACT.Square)
            nc.gpsimd.tensor_scalar(out=h[:], in0=h[:], scalar1=gain_t[:, b, t:t + 1], scalar2=0.0, op0=ALU.mult, op1=ALU.add)
            if i >= LAG:
                pick_inked(i - LAG)

        first_stage(0, 0)
        w1_q[0, 1] = quantize_weight(w1_raw[0, 1], scalar_copy, "w1_01")
        first_stage(0, 1)
        w1_q[1, 1] = quantize_weight(w1_raw[1, 1], vector_copy, "w1_11")
        ctx_t = stage.tile([PART, PASSES * PACK + 1, P1], F32, name="ctx_t", offset=SLOT, align_bytes=64)
        for b in range(PASSES):
            nc.sync.dma_start(out=ctx_t[:, b * PACK:(b + 1) * PACK, :],
                              in_=ctx[b * KP:(b + 1) * KP, :].rearrange("(p t) j -> p t j", t=PACK))
        first_stage(0, 2)
        first_stage(0, 3)
        ws_p = keep.tile([PART, PASSES * H], U32, name="ws_p", align_bytes=64)
        nc.vector.tensor_copy(out=ws_p[:].bitcast(I32).rearrange("p (g t m) -> p g m t", t=PACK, m=PART),
                              in_=ws_raw[:].bitcast(I32).rearrange("p a (b m t) -> p (a b) m t", t=PACK, m=PART))
        first_stage(1, 0)
        first_stage(1, 1)
        quantize_columns(x1[:, 0:PACK, :], 0, P1, scalar_copy, x1_codes[0], x1_plane[0], "x1_bf0")
        first_stage(1, 2)
        first_stage(1, 3)
        for i in range(PASSES * PACK - LAG, PASSES * PACK):
            pick_inked(i)
        quantize_columns(x1[:, PACK:2 * PACK, :], 0, P1 // 2, vector_copy, x1_codes[1], x1_plane[1], "x1_bf1a")
        quantize_columns(x1[:, PACK:2 * PACK, :], P1 // 2, P1 // 2, scalar_copy, x1_codes[1], x1_plane[1], "x1_bf1b")

        wo_raw = [load_rows(wo, a, 0, f"wo_raw{a}", 12 + 2 * a) for a in range(PASSES)]
        board_t = keep.tile([PART, PACK, P2], F32, name="board_t", tag="w1_11_codes", align_bytes=64)
        nc.sync.dma_start(out=board_t[:], in_=board.rearrange("(p t) j -> p t j", t=PACK))

        x3_codes = [keep.tile([PART, P2], U32, name=f"x3_codes{b}", align_bytes=64) for b in range(PASSES)]
        x3_plane = [keep.tile([PART, P2], U8, name=f"x3_plane{b}", align_bytes=64) for b in range(PASSES)]

        x2_tiles = {}

        def pick_contested(i):
            nc.vector.tensor_copy(out=ctx_t[:, i + 1, 0:P2], in_=x2_tiles[i][:].indirect(pos2_t[:]))

        def second_stage(b, t):
            step = psum.tile([PART, P1], F32, name="step", tag="mark")
            for a in range(PASSES):
                c0 = a * H + b * KP + t * PART
                nc.tensor.matmul_mx(out=step[:], lhsT=ws_p[:, c0:c0 + PART].bitcast(FP8X4), lhsT_scale=wsc[4:PART, c0:c0 + PART],
                                    rhs=x1_codes[a][:].bitcast(FP8X4), rhs_scale=x1_plane[a][:],
                                    start=(a == 0), stop=(a == PASSES - 1))
            x2 = ring.tile([PART, P1], F32, name="x2", tag="x2", bufs=LAG + 2)
            i = b * PACK + t
            nc.vector.tensor_tensor(out=x2[:], in0=ctx_t[:, i, :], in1=step[:], op=ALU.mult)
            if i >= LAG:
                pick_contested(i - LAG)
            adder = nc.vector if i == PASSES * PACK - 1 else nc.gpsimd
            adder.tensor_tensor(out=x2[:], in0=x2[:], in1=x1[:, i, :], op=ALU.add)
            x2_tiles[i] = x2

        for t in range(PACK):
            second_stage(0, t)
        wo_q = [quantize_weight(wo_raw[a], scalar_copy, f"wo_{a}") for a in range(PASSES)]
        half_board = keep.tile([PART, PACK, P2], F32, name="half_board")
        nc.scalar.activation(out=half_board[:], in_=board_t[:], func=ACT.Copy, scale=0.5)
        second_stage(1, 0)
        second_stage(1, 1)
        quantize_columns(ctx_t[:, 1:1 + PACK, :], 0, P2, scalar_copy, x3_codes[0], x3_plane[0], "x3_bf0")
        scores = [psum.tile([PART, P2], F32, name=f"score{t}", tag="ground") for t in range(PACK)]

        def score_pass(t, a):
            codes, plane = wo_q[a]
            nc.tensor.matmul_mx(out=scores[t][:], lhsT=codes[:, t * PART:(t + 1) * PART].bitcast(FP8X4),
                                lhsT_scale=plane[:, t * PART:(t + 1) * PART],
                                rhs=x3_codes[a][:].bitcast(FP8X4), rhs_scale=x3_plane[a][:],
                                start=(a == 0), stop=(a == PASSES - 1))

        second_stage(1, 2)
        second_stage(1, 3)
        for t in range(PACK):
            score_pass(t, 0)
        for i in range(PASSES * PACK - LAG, PASSES * PACK):
            pick_contested(i)
        quantize_columns(ctx_t[:, 1 + PACK:1 + 2 * PACK, :], 0, P2, vector_copy, x3_codes[1], x3_plane[1], "x3_bf1")

        out_rows = out.rearrange("(p t) j -> p t j", t=PACK)
        for pair in range(2):
            result = ring.tile([PART, 2, P2], F32, name="result", tag="result")
            for u in range(2):
                t = 2 * pair + u
                score_pass(t, 1)
                nc.scalar.activation(out=result[:, u, :], in_=scores[t][:], func=ACT.Tanh, scale=0.5)
                nc.vector.scalar_tensor_tensor(out=result[:, u, :], in0=result[:, u, :], scalar=1.0, in1=half_board[:, t, :],
                                               op0=ALU.add, op1=ALU.mult)
            nc.sync.dma_start(out=out_rows[:, 2 * pair:2 * pair + 2, :], in_=result[:])
